import numpy as np
import ml_dtypes


def mxq(x, axis, fmt="e4m3"):
    dtype, down = {"e4m3": (ml_dtypes.float8_e4m3fn, 7), "e5m2": (ml_dtypes.float8_e5m2, 14)}[fmt]
    v = np.moveaxis(np.asarray(x, np.float32).astype(ml_dtypes.bfloat16).astype(np.float64), axis, -1)
    blocks = v.reshape(v.shape[:-1] + (-1, 32))
    amax = np.abs(blocks).max(-1, keepdims=True)
    byte = np.maximum(np.where(amax > 0, np.frexp(amax)[1] - 1 + 127, 0) - down, 1)
    scale = np.exp2(byte - 127.0)
    codes = (blocks / scale).astype(np.float32).astype(dtype).astype(np.float64)
    return np.moveaxis((codes * scale).reshape(v.shape), -1, axis)


WIDE = False


def mx_kscale(k):
    if not WIDE:
        return np.ones(k)
    levels = np.array([30, -30])
    if k % 512:
        return np.exp2(np.random.permutation(np.resize(levels, k // 32))).repeat(32)
    a = np.empty((k // 512, 16))
    for p in range(k // 512):
        a[p, :8] = np.random.permutation(np.resize(levels, 8))
        for g in range(8):
            far = levels[np.abs(levels - a[p, g]) >= 10]
            a[p, g + 8] = far[np.random.randint(len(far))]
    return np.exp2(a.ravel()).repeat(32)


def f64(x):
    return np.asarray(x).astype(np.float64)


def striped(idx):
    return np.tile(np.asarray(idx).reshape(-1, 16).T, (8, 1)).astype(np.uint16)


def unstriped(offs):
    return offs[:16].T.reshape(-1).astype(np.int64)


E2M1 = np.array([0.0, 0.5, 1.0, 1.5, 2.0, 3.0, 4.0, 6.0, -0.0, -0.5, -1.0, -1.5, -2.0, -3.0, -4.0, -6.0])


def pack_weight(w, fmt):
    k, n = w.shape
    w = f64(np.asarray(w, np.float32).astype(ml_dtypes.bfloat16)).reshape(k // 32, 32, n)
    amax = np.abs(w).max(1)
    if fmt in ("e4m3", "e5m2"):
        byte = np.frexp(amax)[1] - 1 + 127 - (7 if fmt == "e4m3" else 14)
    else:
        mant, ex = np.frexp(amax / 6.0)
        byte = np.where(mant > 0.5, ex, ex - 1) + 127
    byte = np.clip(np.where(amax > 0, byte, 1), 1, 254)
    scaled = (w * np.exp2(127.0 - byte)[:, None, :]).reshape(k, n).astype(np.float32)
    by_word = np.ascontiguousarray(scaled.reshape(k // 512, 128, 4, n).transpose(0, 1, 3, 2))
    if fmt in ("e4m3", "e5m2"):
        words = by_word.astype(ml_dtypes.float8_e4m3fn if fmt == "e4m3" else ml_dtypes.float8_e5m2).view(np.uint8)
    else:
        c = by_word.astype(ml_dtypes.float4_e2m1fn).view(np.uint8) & 0xF
        words = (c[..., 0::2] | (c[..., 1::2] << 4)).reshape(k // 512, 128, 2 * n)
    return np.ascontiguousarray(words), np.ascontiguousarray(byte.astype(np.uint8).reshape(k // 512, 16, n))


def unpack_weight(words, scales, fmt):
    g, _, n = scales.shape
    words = np.ascontiguousarray(words).reshape(g, 128, n, -1)
    if fmt in ("e4m3", "e5m2"):
        vals = words.view(ml_dtypes.float8_e4m3fn if fmt == "e4m3" else ml_dtypes.float8_e5m2).astype(np.float64)
    else:
        nib = np.empty((g, 128, n, 4), np.uint8)
        nib[..., 0::2] = words & 0xF
        nib[..., 1::2] = words >> 4
        vals = E2M1[nib]
    vals = vals * np.repeat(np.exp2(scales.astype(np.float64) - 127.0), 8, axis=1)[..., None]
    return vals.transpose(0, 1, 3, 2).reshape(g * 512, n)


K, T, J, I, R, Q = 512, 512, 256, 256, 512, 1024


def setup_inputs():
    n = np.random.standard_normal
    idx = np.random.permutation(T)[:J]
    idx2 = np.random.permutation(T)[:I]
    idx3 = np.random.permutation(Q)[:I]
    fk = mx_kscale(K)
    fr = mx_kscale(R)
    xtp = pack_weight(n((K, T)) / fk[:, None], "e2m1")
    wap = pack_weight(n((K, R)) * 0.5 / np.sqrt(K) * fk[:, None] * fr, "e5m2")
    wbp = pack_weight(n((K, R)) * 1 / np.sqrt(K) * fk[:, None] / fr, "e4m3")
    return {
        "xt_words": xtp[0],
        "xt_scales": xtp[1],
        "wa_words": wap[0],
        "wa_scales": wap[1],
        "oa": (n((R, J)) * 0.5 * fr[:, None]).astype(np.float32),
        "wb_words": wbp[0],
        "wb_scales": wbp[1],
        "old": (10.0 * n((J, Q))).astype(np.float32),
        "offs": striped(idx),
        "offs2": striped(idx2),
        "offs3": striped(idx3),
    }


def reference(xt_words, xt_scales, wa_words, wa_scales, oa, wb_words, wb_scales, old, offs, offs2, offs3):
    idx = unstriped(offs)
    idx2 = unstriped(offs2)
    idx3 = unstriped(offs3)
    xtu = unpack_weight(xt_words, xt_scales, "e2m1")
    wau = unpack_weight(wa_words, wa_scales, "e5m2")
    wbu = unpack_weight(wb_words, wb_scales, "e4m3")
    xtidxg = xtu[:, idx]
    za = wau.T @ xtidxg
    ha = np.maximum(za, f64(oa))
    xtidx2g = xtu[:, idx2]
    zb = wbu.T @ xtidx2g
    yb1 = np.pad(zb, ((0, 0), (1, 0)))[:, :I]
    hb = zb - 0.6 * yb1
    haq = mxq(ha, 0, "e5m2")
    hbq = mxq(hb, 0, "e5m2")
    a0 = haq.T @ hbq
    pp = np.zeros((J, Q))
    pp[:, idx3] = a0
    y = 0.04 * (pp - f64(old))
    return y

@@ -1,0 +1,181 @@
+from contextlib import ExitStack
+
+import concourse.mybir as mybir
+
+K, T, J, I, R, Q = 512, 512, 256, 256, 512, 1024
+FLOPS = 2 * K * R * J + 2 * K * R * I + 2 * R * J * I
+
+F32 = mybir.dt.float32
+BF16 = mybir.dt.bfloat16
+I32 = mybir.dt.int32
+U32 = mybir.dt.uint32
+U16 = mybir.dt.uint16
+U8 = mybir.dt.uint8
+E4M3 = mybir.dt.float8_e4m3fn_x4
+E5M2 = mybir.dt.float8_e5m2_x4
+E2M1 = mybir.dt.float4_e2m1fn_x4
+ALU = mybir.AluOpType
+COPY = mybir.ActivationFunctionType.Copy
+
+P = 128
+PACK = 4
+HALF = 128
+LAG = 0.6
+GAIN = 0.04
+CHUNKS = (((0, 512), (512, 512)), ((0, 512), (512, 256), (768, 256)))
+
+
+def tile_list_meet_added_lagged_placed_kernel(
+    tc, xt_words, xt_scales, wa_words, wa_scales, oa, wb_words, wb_scales, old, offs, offs2, offs3, out
+):
+    nc = tc.nc
+    with ExitStack() as ctx:
+        lists = ctx.enter_context(tc.tile_pool(name="lists", bufs=1))
+        sb = ctx.enter_context(tc.tile_pool(name="sb", bufs=1))
+        ps = ctx.enter_context(tc.psum_pool(name="ps", bufs=1))
+
+        def load_scale_rows(queue, plane, scales):
+            for quad in range(4):
+                queue.dma_start(
+                    out=plane[32 * quad : 32 * quad + 4, :].bitcast(I32),
+                    in_=scales[0, 4 * quad : 4 * quad + 4, :].bitcast(I32),
+                )
+
+        def load_words(words_sb, words):
+            nc.sync.dma_start(
+                out=words_sb[:].bitcast(I32), in_=words[0].rearrange("p n t -> p (n t)").bitcast(I32)
+            )
+
+        def deal_columns(dealt, raw, run):
+            nc.scalar.copy(
+                out=dealt.rearrange("p (t g e) -> p t g e", t=PACK, e=run),
+                in_=raw.rearrange("p (g t e) -> p t g e", t=PACK, e=run),
+            )
+
+        x_words = sb.tile([P, T], U16, name="x_words", align_bytes=64)
+        x_scales = sb.tile([P, T], U8, name="x_scales", align_bytes=64)
+        wb_raw = sb.tile([P, R], U32, name="wb_raw", align_bytes=64)
+        wa_raw = sb.tile([P, R], U32, name="wa_raw", align_bytes=64)
+        wb_scales_raw = sb.tile([P, R], U8, name="wb_scales_raw", align_bytes=64)
+        wa_scales_raw = sb.tile([P, R], U8, name="wa_scales_raw", align_bytes=64)
+        list_a = lists.tile([P, J // 16], U16, name="list_a")
+        list_b = lists.tile([P, I // 16], U16, name="list_b")
+        list_q = lists.tile([P, I // 16], U16, name="list_q")
+        oa_sb = sb.tile([P, PACK, J], F32, name="oa_sb", align_bytes=64)
+        old_sb = [sb.tile([P, Q], F32, name="old%d" % h, align_bytes=64) for h in range(2)]
+        pages = [sb.tile([P, Q], F32, name="page%d" % h, align_bytes=64) for h in range(2)]
+        zb_sb = sb.tile([P, (I + 1) * PACK], F32, name="zb_sb", align_bytes=64)
+
+        nc.vector.memset(x_scales[:].bitcast(U32), 0)
+        nc.vector.memset(wb_scales_raw[:].bitcast(U32), 0)
+        nc.vector.memset(wa_scales_raw[:].bitcast(U32), 0)
+        nc.vector.memset(pages[0][:], 0.0)
+        nc.gpsimd.memset(pages[1][:], 0.0)
+        nc.scalar.activation(zb_sb[:, 0:PACK], pages[0][:, 0:PACK], COPY)
+
+        nc.sync.dma_start(out=x_words[:].bitcast(I32), in_=xt_words[0].bitcast(I32))
+        nc.sync.dma_start(list_b[:], offs2)
+        load_scale_rows(nc.scalar, x_scales, xt_scales)
+        nc.sync.dma_start(list_a[:], offs)
+        load_words(wb_raw, wb_words)
+        load_scale_rows(nc.scalar, wb_scales_raw, wb_scales)
+        load_words(wa_raw, wa_words)
+        load_scale_rows(nc.sync, wa_scales_raw, wa_scales)
+        oa_rows = oa.rearrange("(g t e) j -> t g e j", t=PACK, e=8)
+        for t in range(PACK):
+            nc.sync.dma_start(out=oa_sb[:, t, :], in_=oa_rows[t])
+        nc.sync.dma_start(list_q[:], offs3)
+        for h in range(2):
+            nc.sync.dma_start(out=old_sb[h][:], in_=old[h * P : (h + 1) * P, :])
+
+        xb_words = sb.tile([P, I], U16, name="xb_words", align_bytes=64)
+        xb_scales = sb.tile([P, I], U8, name="xb_scales", align_bytes=64)
+        xa_words = sb.tile([P, J], U16, name="xa_words", align_bytes=64)
+        xa_scales = sb.tile([P, J], U8, name="xa_scales", align_bytes=64)
+        nc.vector.tensor_copy(xb_words[:], x_words[:].indirect(list_b[:]))
+        nc.vector.tensor_copy(xb_scales[:], x_scales[:].indirect(list_b[:]))
+        nc.vector.tensor_copy(xa_words[:], x_words[:].indirect(list_a[:]))
+        nc.vector.tensor_copy(xa_scales[:], x_scales[:].indirect(list_a[:]))
+
+        wb_dealt = sb.tile([P, R], U32, name="wb_dealt", align_bytes=64)
+        wa_dealt = sb.tile([P, R], U32, name="wa_dealt", align_bytes=64)
+        wb_scales_dealt = sb.tile([P, R], U8, name="wb_scales_dealt", align_bytes=64)
+        wa_scales_dealt = sb.tile([P, R], U8, name="wa_scales_dealt", align_bytes=64)
+        deal_columns(wb_dealt[:], wb_raw[:], 8)
+        deal_columns(wb_scales_dealt[:].bitcast(U32), wb_scales_raw[:].bitcast(U32), 2)
+        deal_columns(wa_dealt[:], wa_raw[:], 8)
+        deal_columns(wa_scales_dealt[:].bitcast(U32), wa_scales_raw[:].bitcast(U32), 2)
+
+        def first_stage(bank, w_dealt, w_scales_dealt, w_dtype, tok_words, tok_scales, h):
+            cols = slice(h * HALF, (h + 1) * HALF)
+            for t in range(PACK):
+                feats = slice(t * P, (t + 1) * P)
+                nc.tensor.matmul_mx(
+                    out=bank[:, t, :],
+                    lhsT=w_dealt[:, feats].bitcast(w_dtype),
+                    lhsT_scale=w_scales_dealt[:, feats],
+                    rhs=tok_words[:, cols].bitcast(E2M1),
+                    rhs_scale=tok_scales[:, cols],
+                    start=True,
+                    stop=True,
+                )
+
+        hb = sb.tile([P, I * PACK], BF16, name="hb", align_bytes=64)
+        span = HALF * PACK
+        for h in range(2):
+            zb = ps.tile([P, PACK, HALF], F32, name="zb%d" % h)
+            first_stage(zb, wb_dealt, wb_scales_dealt, E4M3, xb_words, xb_scales, h)
+            here = slice(PACK + h * span, PACK + (h + 1) * span)
+            before = slice(h * span, (h + 1) * span)
+            nc.scalar.copy(
+                out=zb_sb[:, here].rearrange("p (i t) -> p i t", t=PACK),
+                in_=zb[:].rearrange("p t i -> p i t"),
+            )
+            nc.vector.scalar_tensor_tensor(
+                out=hb[:, before], in0=zb_sb[:, before], scalar=-LAG, in1=zb_sb[:, here], op0=ALU.mult, op1=ALU.add
+            )
+        hb_codes = sb.tile([P, I], U32, name="hb_codes", align_bytes=64)
+        hb_scales = sb.tile([P, I], U8, name="hb_scales", align_bytes=64)
+
+        scores = [sb.tile([P, I], F32, name="scores%d" % h, align_bytes=64) for h in range(2)]
+        for h in range(2):
+            za = ps.tile([P, PACK, HALF], F32, name="za%d" % h)
+            first_stage(za, wa_dealt, wa_scales_dealt, E5M2, xa_words, xa_scales, h)
+            ha = sb.tile([P, HALF * PACK], BF16, name="ha", align_bytes=64)
+            nc.vector.tensor_tensor(
+                out=ha[:].rearrange("p (j t) -> p j t", t=PACK),
+                in0=za[:].rearrange("p t j -> p j t"),
+                in1=oa_sb[:, :, h * HALF : (h + 1) * HALF].rearrange("p t j -> p j t"),
+                op=ALU.max,
+            )
+            if h == 0:
+                nc.vector.quantize_mx(out=hb_codes[:].bitcast(E5M2), scales=hb_scales[:], in_=hb[:])
+            ha_codes = sb.tile([P, HALF], U32, name="ha_codes%d" % h, align_bytes=64)
+            ha_scales = sb.tile([P, HALF], U8, name="ha_scales%d" % h, align_bytes=64)
+            nc.vector.quantize_mx(out=ha_codes[:].bitcast(E5M2), scales=ha_scales[:], in_=ha[:])
+            a0 = ps.tile([P, I], F32, name="a0_%d" % h)
+            nc.tensor.matmul_mx(
+                out=a0[:],
+                lhsT=ha_codes[:].bitcast(E5M2),
+                lhsT_scale=ha_scales[:],
+                rhs=hb_codes[:].bitcast(E5M2),
+                rhs_scale=hb_scales[:],
+                start=True,
+                stop=True,
+            )
+            if h == 0:
+                nc.scalar.activation(scores[0][:], a0[:], COPY, scale=GAIN)
+                nc.scalar.activation(pages[0][:].indirect(list_q[:]), scores[0][:], COPY)
+            else:
+                nc.vector.tensor_scalar(out=scores[1][:], in0=a0[:], scalar1=GAIN, scalar2=None, op0=ALU.mult)
+                nc.vector.tensor_copy(pages[1][:].indirect(list_q[:, 0:8]), scores[1][:, 0:HALF])
+                nc.scalar.activation(pages[1][:].indirect(list_q[:, 8:16]), scores[1][:, HALF:I], COPY)
+
+        for h in range(2):
+            for c, width in CHUNKS[h]:
+                cols = slice(c, c + width)
+                res = sb.tile([P, width], F32, name="res%d_%d" % (h, c), align_bytes=64)
+                nc.vector.scalar_tensor_tensor(
+                    out=res[:], in0=old_sb[h][:, cols], scalar=-GAIN, in1=pages[h][:, cols], op0=ALU.mult, op1=ALU.add
+                )
+                nc.sync.dma_start(out=out[h * P : (h + 1) * P, cols], in_=res[:])

@@ -34,12 +34,11 @@ def tile_list_meet_added_lagged_placed_kernel(
         sb = ctx.enter_context(tc.tile_pool(name="sb", bufs=1))
         ps = ctx.enter_context(tc.psum_pool(name="ps", bufs=1))
 
-        def load_scale_rows(queue, plane, scales):
-            for quad in range(4):
-                queue.dma_start(
-                    out=plane[32 * quad : 32 * quad + 4, :].bitcast(I32),
-                    in_=scales[0, 4 * quad : 4 * quad + 4, :].bitcast(I32),
-                )
+        def load_scale_rows(queue, plane, scales, quad):
+            rows = scales[0, 4 * quad : 4 * quad + 4, :].bitcast(I32)
+            queue.dma_start(
+                out=plane[32 * quad : 32 * quad + 32, :].bitcast(I32), in_=rows.unsqueeze(0).to_broadcast([8, 4, 128])
+            )
 
         def load_words(words_sb, words):
             nc.sync.dma_start(
@@ -64,24 +63,24 @@ def tile_list_meet_added_lagged_placed_kernel(
         oa_sb = sb.tile([P, PACK, J], F32, name="oa_sb", align_bytes=64)
         old_sb = [sb.tile([P, Q], F32, name="old%d" % h, align_bytes=64) for h in range(2)]
         pages = [sb.tile([P, Q], F32, name="page%d" % h, align_bytes=64) for h in range(2)]
-        zb_sb = sb.tile([P, (I + 1) * PACK], F32, name="zb_sb", align_bytes=64)
+        zb_sb = sb.tile([P, (I + 1) * PACK], F32, name="zb_sb", tag="staging", align_bytes=64)
 
-        nc.vector.memset(x_scales[:].bitcast(U32), 0)
-        nc.vector.memset(wb_scales_raw[:].bitcast(U32), 0)
-        nc.vector.memset(wa_scales_raw[:].bitcast(U32), 0)
         nc.vector.memset(pages[0][:], 0.0)
         nc.gpsimd.memset(pages[1][:], 0.0)
         nc.scalar.activation(zb_sb[:, 0:PACK], pages[0][:, 0:PACK], COPY)
 
+        oa_rows = oa.rearrange("(g t e) j -> t g e j", t=PACK, e=8)
         nc.sync.dma_start(out=x_words[:].bitcast(I32), in_=xt_words[0].bitcast(I32))
         nc.sync.dma_start(list_b[:], offs2)
-        load_scale_rows(nc.scalar, x_scales, xt_scales)
+        for quad in range(4):
+            load_scale_rows(nc.sync, x_scales, xt_scales, quad)
         nc.sync.dma_start(list_a[:], offs)
         load_words(wb_raw, wb_words)
-        load_scale_rows(nc.scalar, wb_scales_raw, wb_scales)
+        for quad in range(4):
+            load_scale_rows(nc.sync, wb_scales_raw, wb_scales, quad)
         load_words(wa_raw, wa_words)
-        load_scale_rows(nc.sync, wa_scales_raw, wa_scales)
-        oa_rows = oa.rearrange("(g t e) j -> t g e j", t=PACK, e=8)
+        for quad in range(4):
+            load_scale_rows(nc.sync, wa_scales_raw, wa_scales, quad)
         for t in range(PACK):
             nc.sync.dma_start(out=oa_sb[:, t, :], in_=oa_rows[t])
         nc.sync.dma_start(list_q[:], offs3)
@@ -120,9 +119,13 @@ def tile_list_meet_added_lagged_placed_kernel(
                     stop=True,
                 )
 
-        hb = sb.tile([P, I * PACK], BF16, name="hb", align_bytes=64)
         span = HALF * PACK
-        for h in range(2):
+        ha_codes = [sb.tile([P, HALF], U32, name="ha_codes%d" % h, align_bytes=64) for h in range(2)]
+        ha_scales = [sb.tile([P, HALF], U8, name="ha_scales%d" % h, align_bytes=64) for h in range(2)]
+        hb_codes = sb.tile([P, I], U32, name="hb_codes", align_bytes=64)
+        hb_scales = sb.tile([P, I], U8, name="hb_scales", align_bytes=64)
+
+        def lagged_half(h):
             zb = ps.tile([P, PACK, HALF], F32, name="zb%d" % h)
             first_stage(zb, wb_dealt, wb_scales_dealt, E4M3, xb_words, xb_scales, h)
             here = slice(PACK + h * span, PACK + (h + 1) * span)
@@ -131,51 +134,80 @@ def tile_list_meet_added_lagged_placed_kernel(
                 out=zb_sb[:, here].rearrange("p (i t) -> p i t", t=PACK),
                 in_=zb[:].rearrange("p t i -> p i t"),
             )
+            hb = sb.tile([P, span], BF16, name="hb%d" % h, align_bytes=64)
             nc.vector.scalar_tensor_tensor(
-                out=hb[:, before], in0=zb_sb[:, before], scalar=-LAG, in1=zb_sb[:, here], op0=ALU.mult, op1=ALU.add
+                out=hb[:], in0=zb_sb[:, before], scalar=-LAG, in1=zb_sb[:, here], op0=ALU.mult, op1=ALU.add
             )
-        hb_codes = sb.tile([P, I], U32, name="hb_codes", align_bytes=64)
-        hb_scales = sb.tile([P, I], U8, name="hb_scales", align_bytes=64)
+            return hb
 
-        scores = [sb.tile([P, I], F32, name="scores%d" % h, align_bytes=64) for h in range(2)]
-        for h in range(2):
+        def quantise_hb(hb, h):
+            cols = slice(h * HALF, (h + 1) * HALF)
+            nc.vector.quantize_mx(out=hb_codes[:, cols].bitcast(E5M2), scales=hb_scales[:, cols], in_=hb[:])
+
+        def raised_half(h):
             za = ps.tile([P, PACK, HALF], F32, name="za%d" % h)
             first_stage(za, wa_dealt, wa_scales_dealt, E5M2, xa_words, xa_scales, h)
-            ha = sb.tile([P, HALF * PACK], BF16, name="ha", align_bytes=64)
+            ha = sb.tile([P, span], BF16, name="ha%d" % h, tag="staging", align_bytes=64)
             nc.vector.tensor_tensor(
                 out=ha[:].rearrange("p (j t) -> p j t", t=PACK),
                 in0=za[:].rearrange("p t j -> p j t"),
                 in1=oa_sb[:, :, h * HALF : (h + 1) * HALF].rearrange("p t j -> p j t"),
                 op=ALU.max,
             )
-            if h == 0:
-                nc.vector.quantize_mx(out=hb_codes[:].bitcast(E5M2), scales=hb_scales[:], in_=hb[:])
-            ha_codes = sb.tile([P, HALF], U32, name="ha_codes%d" % h, align_bytes=64)
-            ha_scales = sb.tile([P, HALF], U8, name="ha_scales%d" % h, align_bytes=64)
-            nc.vector.quantize_mx(out=ha_codes[:].bitcast(E5M2), scales=ha_scales[:], in_=ha[:])
+            return ha
+
+        def quantise_ha(ha, h):
+            nc.vector.quantize_mx(out=ha_codes[h][:].bitcast(E5M2), scales=ha_scales[h][:], in_=ha[:])
+
+        def second_stage(h):
             a0 = ps.tile([P, I], F32, name="a0_%d" % h)
             nc.tensor.matmul_mx(
                 out=a0[:],
-                lhsT=ha_codes[:].bitcast(E5M2),
-                lhsT_scale=ha_scales[:],
+                lhsT=ha_codes[h][:].bitcast(E5M2),
+                lhsT_scale=ha_scales[h][:],
                 rhs=hb_codes[:].bitcast(E5M2),
                 rhs_scale=hb_scales[:],
                 start=True,
                 stop=True,
             )
-            if h == 0:
-                nc.scalar.activation(scores[0][:], a0[:], COPY, scale=GAIN)
-                nc.scalar.activation(pages[0][:].indirect(list_q[:]), scores[0][:], COPY)
-            else:
-                nc.vector.tensor_scalar(out=scores[1][:], in0=a0[:], scalar1=GAIN, scalar2=None, op0=ALU.mult)
-                nc.vector.tensor_copy(pages[1][:].indirect(list_q[:, 0:8]), scores[1][:, 0:HALF])
-                nc.scalar.activation(pages[1][:].indirect(list_q[:, 8:16]), scores[1][:, HALF:I], COPY)
+            return a0
 
+        entry_halves = [(slice(0, HALF), slice(0, 8)), (slice(HALF, I), slice(8, 16))]
+        scores = [
+            [sb.tile([P, HALF], F32, name="scores%d_%d" % (h, e), align_bytes=64) for e in range(2)] for h in range(2)
+        ]
+        hb_halves = [lagged_half(h) for h in range(2)]
+        quantise_hb(hb_halves[0], 0)
+        ha = raised_half(0)
+        quantise_hb(hb_halves[1], 1)
+        quantise_ha(ha, 0)
+        a0 = second_stage(0)
+        for e in range(2):
+            nc.scalar.activation(scores[0][e][:], a0[:, entry_halves[e][0]], COPY, scale=GAIN)
+        for e in range(2):
+            nc.scalar.activation(pages[0][:].indirect(list_q[:, entry_halves[e][1]]), scores[0][e][:], COPY)
+        quantise_ha(raised_half(1), 1)
+        a0 = second_stage(1)
+        for e in range(2):
+            nc.vector.tensor_scalar(
+                out=scores[1][e][:], in0=a0[:, entry_halves[e][0]], scalar1=GAIN, scalar2=None, op0=ALU.mult
+            )
+        nc.vector.tensor_copy(pages[1][:].indirect(list_q[:, entry_halves[0][1]]), scores[1][0][:])
+        nc.scalar.activation(pages[1][:].indirect(list_q[:, entry_halves[1][1]]), scores[1][1][:], COPY)
+
+        results = [
+            sb.tile([P, Q], F32, name="result0", tag="scores1_0", align_bytes=64),
+            sb.tile([P, Q], F32, name="result1", align_bytes=64),
+        ]
         for h in range(2):
             for c, width in CHUNKS[h]:
                 cols = slice(c, c + width)
-                res = sb.tile([P, width], F32, name="res%d_%d" % (h, c), align_bytes=64)
                 nc.vector.scalar_tensor_tensor(
-                    out=res[:], in0=old_sb[h][:, cols], scalar=-GAIN, in1=pages[h][:, cols], op0=ALU.mult, op1=ALU.add
+                    out=results[h][:, cols],
+                    in0=old_sb[h][:, cols],
+                    scalar=-GAIN,
+                    in1=pages[h][:, cols],
+                    op0=ALU.mult,
+                    op1=ALU.add,
                 )
-                nc.sync.dma_start(out=out[h * P : (h + 1) * P, cols], in_=res[:])
+                nc.sync.dma_start(out=out[h * P : (h + 1) * P, cols], in_=results[h][:, cols])

@@ -34,8 +34,8 @@ def tile_list_meet_added_lagged_placed_kernel(
         sb = ctx.enter_context(tc.tile_pool(name="sb", bufs=1))
         ps = ctx.enter_context(tc.psum_pool(name="ps", bufs=1))
 
-        def load_scale_rows(queue, plane, scales, quad):
-            rows = scales[0, 4 * quad : 4 * quad + 4, :].bitcast(I32)
+        def load_scale_rows(queue, plane, source, quad):
+            rows = source[0, 4 * quad : 4 * quad + 4, :].bitcast(I32)
             queue.dma_start(
                 out=plane[32 * quad : 32 * quad + 32, :].bitcast(I32), in_=rows.unsqueeze(0).to_broadcast([8, 4, 128])
             )
@@ -45,8 +45,8 @@ def tile_list_meet_added_lagged_placed_kernel(
                 out=words_sb[:].bitcast(I32), in_=words[0].rearrange("p n t -> p (n t)").bitcast(I32)
             )
 
-        def deal_columns(dealt, raw, run):
-            nc.scalar.copy(
+        def deal_columns(copy, dealt, raw, run):
+            copy(
                 out=dealt.rearrange("p (t g e) -> p t g e", t=PACK, e=run),
                 in_=raw.rearrange("p (g t e) -> p t g e", t=PACK, e=run),
             )
@@ -63,8 +63,9 @@ def tile_list_meet_added_lagged_placed_kernel(
         oa_sb = sb.tile([P, PACK, J], F32, name="oa_sb", align_bytes=64)
         old_sb = [sb.tile([P, Q], F32, name="old%d" % h, align_bytes=64) for h in range(2)]
         pages = [sb.tile([P, Q], F32, name="page%d" % h, align_bytes=64) for h in range(2)]
-        zb_sb = sb.tile([P, (I + 1) * PACK], F32, name="zb_sb", tag="staging", align_bytes=64)
+        zb_sb = sb.tile([P, (I + 1) * PACK], F32, name="zb_sb", align_bytes=64)
 
+        load_scale_rows(nc.gpsimd, wa_scales_raw, wa_scales, 3)
         nc.vector.memset(pages[0][:], 0.0)
         nc.gpsimd.memset(pages[1][:], 0.0)
         nc.scalar.activation(zb_sb[:, 0:PACK], pages[0][:, 0:PACK], COPY)
@@ -79,7 +80,7 @@ def tile_list_meet_added_lagged_placed_kernel(
         for quad in range(4):
             load_scale_rows(nc.sync, wb_scales_raw, wb_scales, quad)
         load_words(wa_raw, wa_words)
-        for quad in range(4):
+        for quad in range(3):
             load_scale_rows(nc.sync, wa_scales_raw, wa_scales, quad)
         for t in range(PACK):
             nc.sync.dma_start(out=oa_sb[:, t, :], in_=oa_rows[t])
@@ -99,13 +100,14 @@ def tile_list_meet_added_lagged_placed_kernel(
         wb_dealt = sb.tile([P, R], U32, name="wb_dealt", align_bytes=64)
         wa_dealt = sb.tile([P, R], U32, name="wa_dealt", align_bytes=64)
         wb_scales_dealt = sb.tile([P, R], U8, name="wb_scales_dealt", align_bytes=64)
-        wa_scales_dealt = sb.tile([P, R], U8, name="wa_scales_dealt", align_bytes=64)
-        deal_columns(wb_dealt[:], wb_raw[:], 8)
-        deal_columns(wb_scales_dealt[:].bitcast(U32), wb_scales_raw[:].bitcast(U32), 2)
-        deal_columns(wa_dealt[:], wa_raw[:], 8)
-        deal_columns(wa_scales_dealt[:].bitcast(U32), wa_scales_raw[:].bitcast(U32), 2)
+        wa_scales_dealt = sb.tile([P, R], U8, name="wa_scales_dealt", tag="wa_raw", align_bytes=64)
+        deal_columns(nc.scalar.copy, wb_dealt[:], wb_raw[:], 8)
+        deal_columns(nc.scalar.copy, wb_scales_dealt[:].bitcast(U32), wb_scales_raw[:].bitcast(U32), 2)
+        deal_columns(nc.vector.tensor_copy, wa_dealt[:].bitcast(I32), wa_raw[:].bitcast(I32), 8)
+        deal_columns(nc.vector.tensor_copy, wa_scales_dealt[:].bitcast(I32), wa_scales_raw[:].bitcast(I32), 2)
 
-        def first_stage(bank, w_dealt, w_scales_dealt, w_dtype, tok_words, tok_scales, h):
+        def first_stage(name, w_dealt, w_scales_dealt, w_dtype, tok_words, tok_scales, h):
+            bank = ps.tile([P, PACK, HALF], F32, name=name)
             cols = slice(h * HALF, (h + 1) * HALF)
             for t in range(PACK):
                 feats = slice(t * P, (t + 1) * P)
@@ -118,96 +120,83 @@ def tile_list_meet_added_lagged_placed_kernel(
                     start=True,
                     stop=True,
                 )
+            return bank
 
         span = HALF * PACK
-        ha_codes = [sb.tile([P, HALF], U32, name="ha_codes%d" % h, align_bytes=64) for h in range(2)]
-        ha_scales = [sb.tile([P, HALF], U8, name="ha_scales%d" % h, align_bytes=64) for h in range(2)]
-        hb_codes = sb.tile([P, I], U32, name="hb_codes", align_bytes=64)
-        hb_scales = sb.tile([P, I], U8, name="hb_scales", align_bytes=64)
+        codes = sb.tile([P, J + I], U32, name="codes", align_bytes=64)
+        scales = sb.tile([P, J + I], U8, name="scales", align_bytes=64)
+        ha_first = (0, HALF + I)
+        hb_first = HALF
 
-        def lagged_half(h):
-            zb = ps.tile([P, PACK, HALF], F32, name="zb%d" % h)
-            first_stage(zb, wb_dealt, wb_scales_dealt, E4M3, xb_words, xb_scales, h)
+        def hidden_half(h):
+            staging = sb.tile([P, 2 * span], BF16, name="staging", tag="wa_scales_raw", align_bytes=64)
             here = slice(PACK + h * span, PACK + (h + 1) * span)
             before = slice(h * span, (h + 1) * span)
             nc.scalar.copy(
                 out=zb_sb[:, here].rearrange("p (i t) -> p i t", t=PACK),
-                in_=zb[:].rearrange("p t i -> p i t"),
+                in_=zb[h][:].rearrange("p t i -> p i t"),
             )
-            hb = sb.tile([P, span], BF16, name="hb%d" % h, align_bytes=64)
             nc.vector.scalar_tensor_tensor(
-                out=hb[:], in0=zb_sb[:, before], scalar=-LAG, in1=zb_sb[:, here], op0=ALU.mult, op1=ALU.add
+                out=staging[:, span : 2 * span],
+                in0=zb_sb[:, before],
+                scalar=-LAG,
+                in1=zb_sb[:, here],
+                op0=ALU.mult,
+                op1=ALU.add,
             )
-            return hb
-
-        def quantise_hb(hb, h):
-            cols = slice(h * HALF, (h + 1) * HALF)
-            nc.vector.quantize_mx(out=hb_codes[:, cols].bitcast(E5M2), scales=hb_scales[:, cols], in_=hb[:])
-
-        def raised_half(h):
-            za = ps.tile([P, PACK, HALF], F32, name="za%d" % h)
-            first_stage(za, wa_dealt, wa_scales_dealt, E5M2, xa_words, xa_scales, h)
-            ha = sb.tile([P, span], BF16, name="ha%d" % h, tag="staging", align_bytes=64)
             nc.vector.tensor_tensor(
-                out=ha[:].rearrange("p (j t) -> p j t", t=PACK),
-                in0=za[:].rearrange("p t j -> p j t"),
-                in1=oa_sb[:, :, h * HALF : (h + 1) * HALF].rearrange("p t j -> p j t"),
+                out=staging[:, 0:span].rearrange("p (c i t) -> p c t i", t=PACK, i=2),
+                in0=za[h][:].rearrange("p t (c i) -> p c t i", i=2),
+                in1=oa_sb[:, :, h * HALF : (h + 1) * HALF].rearrange("p t (c i) -> p c t i", i=2),
                 op=ALU.max,
             )
-            return ha
+            return staging
 
-        def quantise_ha(ha, h):
-            nc.vector.quantize_mx(out=ha_codes[h][:].bitcast(E5M2), scales=ha_scales[h][:], in_=ha[:])
+        def quantise(values, first, count):
+            cols = slice(first, first + count)
+            nc.vector.quantize_mx(out=codes[:, cols].bitcast(E5M2), scales=scales[:, cols], in_=values)
 
-        def second_stage(h):
-            a0 = ps.tile([P, I], F32, name="a0_%d" % h)
+        def scaled_scores(h, first, count):
+            rows = slice(ha_first[h], ha_first[h] + HALF)
+            cols = slice(hb_first + first, hb_first + first + count)
+            a0 = ps.tile([P, count], F32, name="a0_%d_%d" % (h, first))
             nc.tensor.matmul_mx(
                 out=a0[:],
-                lhsT=ha_codes[h][:].bitcast(E5M2),
-                lhsT_scale=ha_scales[h][:],
-                rhs=hb_codes[:].bitcast(E5M2),
-                rhs_scale=hb_scales[:],
+                lhsT=codes[:, rows].bitcast(E5M2),
+                lhsT_scale=scales[:, rows],
+                rhs=codes[:, cols].bitcast(E5M2),
+                rhs_scale=scales[:, cols],
                 start=True,
                 stop=True,
             )
-            return a0
+            scores = sb.tile([P, count], F32, name="scores%d_%d" % (h, first), align_bytes=64)
+            nc.scalar.activation(scores[:], a0[:], COPY, scale=GAIN)
+            return scores
 
-        entry_halves = [(slice(0, HALF), slice(0, 8)), (slice(HALF, I), slice(8, 16))]
-        scores = [
-            [sb.tile([P, HALF], F32, name="scores%d_%d" % (h, e), align_bytes=64) for e in range(2)] for h in range(2)
-        ]
-        hb_halves = [lagged_half(h) for h in range(2)]
-        quantise_hb(hb_halves[0], 0)
-        ha = raised_half(0)
-        quantise_hb(hb_halves[1], 1)
-        quantise_ha(ha, 0)
-        a0 = second_stage(0)
-        for e in range(2):
-            nc.scalar.activation(scores[0][e][:], a0[:, entry_halves[e][0]], COPY, scale=GAIN)
-        for e in range(2):
-            nc.scalar.activation(pages[0][:].indirect(list_q[:, entry_halves[e][1]]), scores[0][e][:], COPY)
-        quantise_ha(raised_half(1), 1)
-        a0 = second_stage(1)
-        for e in range(2):
-            nc.vector.tensor_scalar(
-                out=scores[1][e][:], in0=a0[:, entry_halves[e][0]], scalar1=GAIN, scalar2=None, op0=ALU.mult
-            )
-        nc.vector.tensor_copy(pages[1][:].indirect(list_q[:, entry_halves[0][1]]), scores[1][0][:])
-        nc.scalar.activation(pages[1][:].indirect(list_q[:, entry_halves[1][1]]), scores[1][1][:], COPY)
+        zb = [first_stage("zb%d" % h, wb_dealt, wb_scales_dealt, E4M3, xb_words, xb_scales, h) for h in range(2)]
+        za = [first_stage("za%d" % h, wa_dealt, wa_scales_dealt, E5M2, xa_words, xa_scales, h) for h in range(2)]
 
-        results = [
-            sb.tile([P, Q], F32, name="result0", tag="scores1_0", align_bytes=64),
-            sb.tile([P, Q], F32, name="result1", align_bytes=64),
-        ]
+        quantise(hidden_half(0)[:], ha_first[0], 2 * HALF)
+        scores = scaled_scores(0, 0, HALF)
+        nc.scalar.activation(pages[0][:].indirect(list_q[:, 0:8]), scores[:], COPY)
+        staging = hidden_half(1)
+        quantise(staging[:, span : 2 * span], hb_first + HALF, HALF)
+        quantise(staging[:, 0:span], ha_first[1], HALF)
+        scores = scaled_scores(0, HALF, HALF)
+        nc.vector.tensor_copy(pages[0][:].indirect(list_q[:, 8:16]), scores[:])
+        scores = scaled_scores(1, 0, I)
+        nc.scalar.activation(pages[1][:].indirect(list_q[:]), scores[:], COPY)
+
         for h in range(2):
+            result = sb.tile([P, Q], F32, name="result%d" % h, align_bytes=64)
             for c, width in CHUNKS[h]:
                 cols = slice(c, c + width)
                 nc.vector.scalar_tensor_tensor(
-                    out=results[h][:, cols],
+                    out=result[:, cols],
                     in0=old_sb[h][:, cols],
                     scalar=-GAIN,
                     in1=pages[h][:, cols],
                     op0=ALU.mult,
                     op1=ALU.add,
                 )
-                nc.sync.dma_start(out=out[h * P : (h + 1) * P, cols], in_=results[h][:, cols])
+                nc.sync.dma_start(out=out[h * P : (h + 1) * P, cols], in_=result[:, cols])

from contextlib import ExitStack

import concourse.mybir as mybir

K, T, J, I, R, Q = 512, 512, 256, 256, 512, 1024
FLOPS = 2 * K * R * J + 2 * K * R * I + 2 * R * J * I

F32 = mybir.dt.float32
BF16 = mybir.dt.bfloat16
I32 = mybir.dt.int32
U32 = mybir.dt.uint32
U16 = mybir.dt.uint16
U8 = mybir.dt.uint8
E4M3 = mybir.dt.float8_e4m3fn_x4
E5M2 = mybir.dt.float8_e5m2_x4
E2M1 = mybir.dt.float4_e2m1fn_x4
ALU = mybir.AluOpType
COPY = mybir.ActivationFunctionType.Copy

P = 128
PACK = 4
HALF = 128
LAG = 0.6
GAIN = 0.04
CHUNKS = (((0, 512), (512, 512)), ((0, 512), (512, 256), (768, 256)))


def tile_list_meet_added_lagged_placed_kernel(
    tc, xt_words, xt_scales, wa_words, wa_scales, oa, wb_words, wb_scales, old, offs, offs2, offs3, out
):
    nc = tc.nc
    with ExitStack() as ctx:
        lists = ctx.enter_context(tc.tile_pool(name="lists", bufs=1))
        sb = ctx.enter_context(tc.tile_pool(name="sb", bufs=1))
        ps = ctx.enter_context(tc.psum_pool(name="ps", bufs=1))

        def load_scale_rows(queue, plane, source, quad):
            rows = source[0, 4 * quad : 4 * quad + 4, :].bitcast(I32)
            queue.dma_start(
                out=plane[32 * quad : 32 * quad + 32, :].bitcast(I32), in_=rows.unsqueeze(0).to_broadcast([8, 4, 128])
            )

        def load_words(words_sb, words):
            nc.sync.dma_start(
                out=words_sb[:].bitcast(I32), in_=words[0].rearrange("p n t -> p (n t)").bitcast(I32)
            )

        def deal_columns(copy, dealt, raw, run):
            copy(
                out=dealt.rearrange("p (t g e) -> p t g e", t=PACK, e=run),
                in_=raw.rearrange("p (g t e) -> p t g e", t=PACK, e=run),
            )

        x_words = sb.tile([P, T], U16, name="x_words", align_bytes=64)
        x_scales = sb.tile([P, T], U8, name="x_scales", align_bytes=64)
        wb_raw = sb.tile([P, R], U32, name="wb_raw", align_bytes=64)
        wa_raw = sb.tile([P, R], U32, name="wa_raw", align_bytes=64)
        wb_scales_raw = sb.tile([P, R], U8, name="wb_scales_raw", align_bytes=64)
        wa_scales_raw = sb.tile([P, R], U8, name="wa_scales_raw", align_bytes=64)
        list_a = lists.tile([P, J // 16], U16, name="list_a")
        list_b = lists.tile([P, I // 16], U16, name="list_b")
        list_q = lists.tile([P, I // 16], U16, name="list_q")
        oa_sb = sb.tile([P, PACK, J], F32, name="oa_sb", align_bytes=64)
        old_sb = [sb.tile([P, Q], F32, name="old%d" % h, align_bytes=64) for h in range(2)]
        pages = [sb.tile([P, Q], F32, name="page%d" % h, align_bytes=64) for h in range(2)]
        zb_sb = sb.tile([P, (I + 1) * PACK], F32, name="zb_sb", align_bytes=64)

        load_scale_rows(nc.gpsimd, wa_scales_raw, wa_scales, 3)
        nc.vector.memset(pages[0][:], 0.0)
        nc.gpsimd.memset(pages[1][:], 0.0)
        nc.scalar.activation(zb_sb[:, 0:PACK], pages[0][:, 0:PACK], COPY)

        oa_rows = oa.rearrange("(g t e) j -> t g e j", t=PACK, e=8)
        nc.sync.dma_start(out=x_words[:].bitcast(I32), in_=xt_words[0].bitcast(I32))
        nc.sync.dma_start(list_b[:], offs2)
        for quad in range(4):
            load_scale_rows(nc.sync, x_scales, xt_scales, quad)
        nc.sync.dma_start(list_a[:], offs)
        load_words(wb_raw, wb_words)
        for quad in range(4):
            load_scale_rows(nc.sync, wb_scales_raw, wb_scales, quad)
        load_words(wa_raw, wa_words)
        for quad in range(3):
            load_scale_rows(nc.sync, wa_scales_raw, wa_scales, quad)
        for t in range(PACK):
            nc.sync.dma_start(out=oa_sb[:, t, :], in_=oa_rows[t])
        nc.sync.dma_start(list_q[:], offs3)
        for h in range(2):
            nc.sync.dma_start(out=old_sb[h][:], in_=old[h * P : (h + 1) * P, :])

        xb_words = sb.tile([P, I], U16, name="xb_words", align_bytes=64)
        xb_scales = sb.tile([P, I], U8, name="xb_scales", align_bytes=64)
        xa_words = sb.tile([P, J], U16, name="xa_words", align_bytes=64)
        xa_scales = sb.tile([P, J], U8, name="xa_scales", align_bytes=64)
        nc.vector.tensor_copy(xb_words[:], x_words[:].indirect(list_b[:]))
        nc.vector.tensor_copy(xb_scales[:], x_scales[:].indirect(list_b[:]))
        nc.vector.tensor_copy(xa_words[:], x_words[:].indirect(list_a[:]))
        nc.vector.tensor_copy(xa_scales[:], x_scales[:].indirect(list_a[:]))

        wb_dealt = sb.tile([P, R], U32, name="wb_dealt", align_bytes=64)
        wa_dealt = sb.tile([P, R], U32, name="wa_dealt", align_bytes=64)
        wb_scales_dealt = sb.tile([P, R], U8, name="wb_scales_dealt", align_bytes=64)
        wa_scales_dealt = sb.tile([P, R], U8, name="wa_scales_dealt", tag="wa_raw", align_bytes=64)
        deal_columns(nc.scalar.copy, wb_dealt[:], wb_raw[:], 8)
        deal_columns(nc.scalar.copy, wb_scales_dealt[:].bitcast(U32), wb_scales_raw[:].bitcast(U32), 2)
        deal_columns(nc.vector.tensor_copy, wa_dealt[:].bitcast(I32), wa_raw[:].bitcast(I32), 8)
        deal_columns(nc.vector.tensor_copy, wa_scales_dealt[:].bitcast(I32), wa_scales_raw[:].bitcast(I32), 2)

        def first_stage(name, w_dealt, w_scales_dealt, w_dtype, tok_words, tok_scales, h):
            bank = ps.tile([P, PACK, HALF], F32, name=name)
            cols = slice(h * HALF, (h + 1) * HALF)
            for t in range(PACK):
                feats = slice(t * P, (t + 1) * P)
                nc.tensor.matmul_mx(
                    out=bank[:, t, :],
                    lhsT=w_dealt[:, feats].bitcast(w_dtype),
                    lhsT_scale=w_scales_dealt[:, feats],
                    rhs=tok_words[:, cols].bitcast(E2M1),
                    rhs_scale=tok_scales[:, cols],
                    start=True,
                    stop=True,
                )
            return bank

        span = HALF * PACK
        codes = sb.tile([P, J + I], U32, name="codes", align_bytes=64)
        scales = sb.tile([P, J + I], U8, name="scales", align_bytes=64)
        ha_first = (0, HALF + I)
        hb_first = HALF

        def hidden_half(h):
            staging = sb.tile([P, 2 * span], BF16, name="staging", tag="wa_scales_raw", align_bytes=64)
            here = slice(PACK + h * span, PACK + (h + 1) * span)
            before = slice(h * span, (h + 1) * span)
            nc.scalar.copy(
                out=zb_sb[:, here].rearrange("p (i t) -> p i t", t=PACK),
                in_=zb[h][:].rearrange("p t i -> p i t"),
            )
            nc.vector.scalar_tensor_tensor(
                out=staging[:, span : 2 * span],
                in0=zb_sb[:, before],
                scalar=-LAG,
                in1=zb_sb[:, here],
                op0=ALU.mult,
                op1=ALU.add,
            )
            nc.vector.tensor_tensor(
                out=staging[:, 0:span].rearrange("p (c i t) -> p c t i", t=PACK, i=2),
                in0=za[h][:].rearrange("p t (c i) -> p c t i", i=2),
                in1=oa_sb[:, :, h * HALF : (h + 1) * HALF].rearrange("p t (c i) -> p c t i", i=2),
                op=ALU.max,
            )
            return staging

        def quantise(values, first, count):
            cols = slice(first, first + count)
            nc.vector.quantize_mx(out=codes[:, cols].bitcast(E5M2), scales=scales[:, cols], in_=values)

        def scaled_scores(h, first, count):
            rows = slice(ha_first[h], ha_first[h] + HALF)
            cols = slice(hb_first + first, hb_first + first + count)
            a0 = ps.tile([P, count], F32, name="a0_%d_%d" % (h, first))
            nc.tensor.matmul_mx(
                out=a0[:],
                lhsT=codes[:, rows].bitcast(E5M2),
                lhsT_scale=scales[:, rows],
                rhs=codes[:, cols].bitcast(E5M2),
                rhs_scale=scales[:, cols],
                start=True,
                stop=True,
            )
            scores = sb.tile([P, count], F32, name="scores%d_%d" % (h, first), align_bytes=64)
            nc.scalar.activation(scores[:], a0[:], COPY, scale=GAIN)
            return scores

        zb = [first_stage("zb%d" % h, wb_dealt, wb_scales_dealt, E4M3, xb_words, xb_scales, h) for h in range(2)]
        za = [first_stage("za%d" % h, wa_dealt, wa_scales_dealt, E5M2, xa_words, xa_scales, h) for h in range(2)]

        quantise(hidden_half(0)[:], ha_first[0], 2 * HALF)
        scores = scaled_scores(0, 0, HALF)
        nc.scalar.activation(pages[0][:].indirect(list_q[:, 0:8]), scores[:], COPY)
        staging = hidden_half(1)
        quantise(staging[:, span : 2 * span], hb_first + HALF, HALF)
        quantise(staging[:, 0:span], ha_first[1], HALF)
        scores = scaled_scores(0, HALF, HALF)
        nc.vector.tensor_copy(pages[0][:].indirect(list_q[:, 8:16]), scores[:])
        scores = scaled_scores(1, 0, I)
        nc.scalar.activation(pages[1][:].indirect(list_q[:]), scores[:], COPY)

        for h in range(2):
            result = sb.tile([P, Q], F32, name="result%d" % h, align_bytes=64)
            for c, width in CHUNKS[h]:
                cols = slice(c, c + width)
                nc.vector.scalar_tensor_tensor(
                    out=result[:, cols],
                    in0=old_sb[h][:, cols],
                    scalar=-GAIN,
                    in1=pages[h][:, cols],
                    op0=ALU.mult,
                    op1=ALU.add,
                )
                nc.sync.dma_start(out=out[h * P : (h + 1) * P, cols], in_=result[:, cols])
